import numpy as np
import ml_dtypes


def mxq(x, axis, fmt="e4m3"):
    dtype, down = {"e4m3": (ml_dtypes.float8_e4m3fn, 7), "e5m2": (ml_dtypes.float8_e5m2, 14)}[fmt]
    v = np.moveaxis(np.asarray(x, np.float32).astype(ml_dtypes.bfloat16).astype(np.float64), axis, -1)
    blocks = v.reshape(v.shape[:-1] + (-1, 32))
    amax = np.abs(blocks).max(-1, keepdims=True)
    byte = np.maximum(np.where(amax > 0, np.frexp(amax)[1] - 1 + 127, 0) - down, 1)
    scale = np.exp2(byte - 127.0)
    codes = (blocks / scale).astype(np.float32).astype(dtype).astype(np.float64)
    return np.moveaxis((codes * scale).reshape(v.shape), -1, axis)


WIDE = False


def mx_kscale(k):
    if not WIDE:
        return np.ones(k)
    levels = np.array([30, -30])
    if k % 512:
        return np.exp2(np.random.permutation(np.resize(levels, k // 32))).repeat(32)
    a = np.empty((k // 512, 16))
    for p in range(k // 512):
        a[p, :8] = np.random.permutation(np.resize(levels, 8))
        for g in range(8):
            far = levels[np.abs(levels - a[p, g]) >= 10]
            a[p, g + 8] = far[np.random.randint(len(far))]
    return np.exp2(a.ravel()).repeat(32)


def f64(x):
    return np.asarray(x).astype(np.float64)


def striped(idx):
    return np.tile(np.asarray(idx).reshape(-1, 16).T, (8, 1)).astype(np.uint16)


def unstriped(offs):
    return offs[:16].T.reshape(-1).astype(np.int64)


E2M1 = np.array([0.0, 0.5, 1.0, 1.5, 2.0, 3.0, 4.0, 6.0, -0.0, -0.5, -1.0, -1.5, -2.0, -3.0, -4.0, -6.0])


def pack_weight(w, fmt):
    k, n = w.shape
    w = f64(np.asarray(w, np.float32).astype(ml_dtypes.bfloat16)).reshape(k // 32, 32, n)
    amax = np.abs(w).max(1)
    if fmt in ("e4m3", "e5m2"):
        byte = np.frexp(amax)[1] - 1 + 127 - (7 if fmt == "e4m3" else 14)
    else:
        mant, ex = np.frexp(amax / 6.0)
        byte = np.where(mant > 0.5, ex, ex - 1) + 127
    byte = np.clip(np.where(amax > 0, byte, 1), 1, 254)
    scaled = (w * np.exp2(127.0 - byte)[:, None, :]).reshape(k, n).astype(np.float32)
    by_word = np.ascontiguousarray(scaled.reshape(k // 512, 128, 4, n).transpose(0, 1, 3, 2))
    if fmt in ("e4m3", "e5m2"):
        words = by_word.astype(ml_dtypes.float8_e4m3fn if fmt == "e4m3" else ml_dtypes.float8_e5m2).view(np.uint8)
    else:
        c = by_word.astype(ml_dtypes.float4_e2m1fn).view(np.uint8) & 0xF
        words = (c[..., 0::2] | (c[..., 1::2] << 4)).reshape(k // 512, 128, 2 * n)
    return np.ascontiguousarray(words), np.ascontiguousarray(byte.astype(np.uint8).reshape(k // 512, 16, n))


def unpack_weight(words, scales, fmt):
    g, _, n = scales.shape
    words = np.ascontiguousarray(words).reshape(g, 128, n, -1)
    if fmt in ("e4m3", "e5m2"):
        vals = words.view(ml_dtypes.float8_e4m3fn if fmt == "e4m3" else ml_dtypes.float8_e5m2).astype(np.float64)
    else:
        nib = np.empty((g, 128, n, 4), np.uint8)
        nib[..., 0::2] = words & 0xF
        nib[..., 1::2] = words >> 4
        vals = E2M1[nib]
    vals = vals * np.repeat(np.exp2(scales.astype(np.float64) - 127.0), 8, axis=1)[..., None]
    return vals.transpose(0, 1, 3, 2).reshape(g * 512, n)


def sigmoid(v):
    return 1.0 / (1.0 + np.exp(-v))


K, F, T, Z, J, R, O, N, L, E = 512, 512, 1024, 1024, 256, 512, 128, 256, 512, 1024


def setup_inputs():
    n = np.random.standard_normal
    idx = np.random.permutation(T)[:J]
    idx2 = np.random.permutation(Z)[:J]
    idx3 = np.random.permutation(J)[:O]
    idx4 = np.random.permutation(J)[:O]
    idx5 = np.random.permutation(E)[:O]
    fk = mx_kscale(K)
    ff = mx_kscale(F)
    fr = mx_kscale(R)
    fl = mx_kscale(L)
    xtp = pack_weight(n((K, T)) / fk[:, None], "e4m3")
    wp = pack_weight(n((K, R)) * 1 / np.sqrt(K) * fk[:, None], "e2m1")
    xop = pack_weight(n((F, Z)) / ff[:, None], "e2m1")
    w2p = pack_weight(n((F, R)) * 1 / np.sqrt(F) * ff[:, None] * fr, "e5m2")
    wbp = pack_weight(n((R, N)) * 1 / np.sqrt(R) / fr[:, None], "e5m2")
    sxp = pack_weight(n((L, O)) / fl[:, None], "e2m1")
    wsp = pack_weight(n((L, N)) * 1 / np.sqrt(L) * fl[:, None], "e5m2")
    return {
        "xt_words": xtp[0],
        "xt_scales": xtp[1],
        "w_words": wp[0],
        "w_scales": wp[1],
        "xo_words": xop[0],
        "xo_scales": xop[1],
        "w2_words": w2p[0],
        "w2_scales": w2p[1],
        "sg": (np.random.uniform(0.6, 1.6, (R, 1))).astype(np.float32),
        "wb_words": wbp[0],
        "wb_scales": wbp[1],
        "sx_words": sxp[0],
        "sx_scales": sxp[1],
        "ws_words": wsp[0],
        "ws_scales": wsp[1],
        "tz": (n((N, E))).astype(np.float32),
        "offs": striped(idx),
        "offs2": striped(idx2),
        "offs3": striped(idx3),
        "offs4": striped(idx4),
        "offs5": striped(idx5),
    }


def reference(xt_words, xt_scales, w_words, w_scales, xo_words, xo_scales, w2_words, w2_scales, sg, wb_words, wb_scales, sx_words, sx_scales, ws_words, ws_scales, tz, offs, offs2, offs3, offs4, offs5):
    idx = unstriped(offs)
    idx2 = unstriped(offs2)
    idx3 = unstriped(offs3)
    idx4 = unstriped(offs4)
    idx5 = unstriped(offs5)
    xtu = unpack_weight(xt_words, xt_scales, "e4m3")
    wu = unpack_weight(w_words, w_scales, "e2m1")
    xou = unpack_weight(xo_words, xo_scales, "e2m1")
    w2u = unpack_weight(w2_words, w2_scales, "e5m2")
    wbu = unpack_weight(wb_words, wb_scales, "e5m2")
    sxu = unpack_weight(sx_words, sx_scales, "e2m1")
    wsu = unpack_weight(ws_words, ws_scales, "e5m2")
    xtidxg = xtu[:, idx]
    a = wu.T @ xtidxg
    xoidx2g = xou[:, idx2]
    b = w2u.T @ xoidx2g
    hid = np.maximum(b[:, idx3], b[:, idx4]) * sigmoid(a[:, idx4] * f64(sg))
    hidq = mxq(hid, 0, "e4m3")
    p = wbu.T @ hidq + wsu.T @ sxu
    y = p + f64(tz)[:, idx5]
    return y

@@ -1,0 +1,198 @@
+from contextlib import ExitStack
+
+import concourse.mybir as mybir
+
+F32 = mybir.dt.float32
+BF16 = mybir.dt.bfloat16
+I32 = mybir.dt.int32
+U32 = mybir.dt.uint32
+U16 = mybir.dt.uint16
+U8 = mybir.dt.uint8
+E4M3X4 = mybir.dt.float8_e4m3fn_x4
+E5M2X4 = mybir.dt.float8_e5m2_x4
+E2M1X4 = mybir.dt.float4_e2m1fn_x4
+ACT = mybir.ActivationFunctionType
+ALU = mybir.AluOpType
+
+P = 128
+PACK = 4
+T, Z, J, R, O, N, E = 1024, 1024, 256, 512, 128, 256, 1024
+FLOPS = 2 * 512 * (R * J * 2 + N * O * 2)
+
+
+def tile_list_twotab_agree_skip_tabled_kernel(
+    tc, xt_words, xt_scales, w_words, w_scales, xo_words, xo_scales, w2_words, w2_scales, sg,
+    wb_words, wb_scales, sx_words, sx_scales, ws_words, ws_scales, tz, offs, offs2, offs3, offs4, offs5, out,
+):
+    nc = tc.nc
+    with ExitStack() as ctx:
+        sb = ctx.enter_context(tc.tile_pool(name="sb", bufs=1))
+        ps = ctx.enter_context(tc.psum_pool(name="ps", bufs=1))
+
+        def tile(name, shape, dtype):
+            return sb.tile(shape, dtype, name=name, align_bytes=64)
+
+        def load_list(name, src):
+            held = tile(name, list(src.shape), U16)
+            nc.sync.dma_start(held[:], src)
+            return held
+
+        def load_words(queue, name, src, cols, dtype):
+            held = tile(name, [P, cols], dtype)
+            flat = src[0] if len(src.shape) == 3 else src[0].rearrange("p n t -> p (n t)")
+            queue.dma_start(held[:].bitcast(I32), flat.bitcast(I32))
+            return held
+
+        def zeroed(engine, name, cols):
+            plane = tile(name, [P, cols], U8)
+            engine.memset(plane[:].bitcast(I32), 0)
+            return plane
+
+        def staged(name, cols):
+            held = tile(name, [P, 4, cols], U8)
+            nc.vector.memset(held[:, 0, :].bitcast(I32), 0)
+            return held
+
+        def load_staged(queue, held, first, src):
+            queue.dma_start(
+                held[0:P:32, :, first : first + src.shape[2]].bitcast(I32),
+                src[0].rearrange("(q r) c -> q r c", r=4).bitcast(I32),
+            )
+
+        def spread_staged(queue, held):
+            for r in range(1, 4):
+                queue.dma_start(held[r:P:32, 0, :].bitcast(I32), held[0:P:32, r, :].bitcast(I32))
+
+        def load_scale_rows(queue, plane, src, r):
+            queue.dma_start(plane[r:P:32, :].bitcast(I32), src[0, r:16:4, :].bitcast(I32))
+
+        early = staged("early", 2 * R)
+        xo_s = zeroed(nc.vector, "xo_s", Z)
+        xt_s = zeroed(nc.vector, "xt_s", T)
+        late = staged("late", N + O + N)
+        w2_s, w_s = early[:, 0, 0:R], early[:, 0, R : 2 * R]
+        ws_s, sx_s, wb_s = late[:, 0, 0:N], late[:, 0, N : N + O], late[:, 0, N + O : N + O + N]
+
+        xt_w = load_words(nc.gpsimd, "xt_w", xt_words, T, U32)
+        load_scale_rows(nc.gpsimd, xt_s, xt_scales, 2)
+        load_scale_rows(nc.gpsimd, xt_s, xt_scales, 3)
+
+        load_staged(nc.scalar, early, 0, w2_scales)
+        load_staged(nc.scalar, early, R, w_scales)
+        load_scale_rows(nc.scalar, xo_s, xo_scales, 0)
+        load_scale_rows(nc.scalar, xo_s, xo_scales, 1)
+        spread_staged(nc.scalar, early)
+
+        l2 = load_list("l2", offs2)
+        xo_w = load_words(nc.sync, "xo_w", xo_words, Z, U16)
+        load_scale_rows(nc.sync, xo_s, xo_scales, 2)
+        load_scale_rows(nc.sync, xo_s, xo_scales, 3)
+        w2_w = load_words(nc.sync, "w2_w", w2_words, R, U32)
+        l1 = load_list("l1", offs)
+        w_w = load_words(nc.sync, "w_w", w_words, R, U16)
+        load_scale_rows(nc.sync, xt_s, xt_scales, 0)
+        load_scale_rows(nc.sync, xt_s, xt_scales, 1)
+        l3 = load_list("l3", offs3)
+        l4 = load_list("l4", offs4)
+        slope = tile("slope", [P, PACK], F32)
+        nc.sync.dma_start(slope[:], sg.rearrange("(p t) o -> p (t o)", t=PACK))
+        load_staged(nc.sync, late, 0, ws_scales)
+        load_staged(nc.sync, late, N, sx_scales)
+        load_staged(nc.sync, late, N + O, wb_scales)
+        tz_sb = tile("tz_sb", [P, 2, E], F32)
+        nc.sync.dma_start(tz_sb[:], tz.rearrange("(h p) e -> p h e", p=P))
+        wb_w = load_words(nc.sync, "wb_w", wb_words, N, U32)
+        ws_w = load_words(nc.sync, "ws_w", ws_words, N, U32)
+        sx_w = load_words(nc.sync, "sx_w", sx_words, O, U16)
+        l5 = load_list("l5", offs5)
+        spread_staged(nc.sync, late)
+
+        def dealt(copy, name, src, dtype, run):
+            held = tile(name, [P, R], dtype)
+            copy(
+                held[:].rearrange("p (t c i) -> p c t i", t=PACK, i=run),
+                src.rearrange("p (c i t) -> p c t i", t=PACK, i=run),
+            )
+            return held
+
+        def gathered(name, window, offsets, dtype):
+            held = tile(name, [P, J], dtype)
+            nc.vector.tensor_copy(held[:], window[:].indirect(offsets[:]))
+            return held
+
+        xo_wg = gathered("xo_wg", xo_w, l2, U16)
+        xo_sg = gathered("xo_sg", xo_s, l2, U8)
+        w2_wd = dealt(nc.scalar.copy, "w2_wd", w2_w[:], U32, 4)
+        w2_sd = dealt(nc.gpsimd.tensor_copy, "w2_sd", w2_s, U8, 16)
+        b_sb = []
+        for u in range(2):
+            bank = ps.tile([P, 2, J], F32, name="b_ps%d" % u)
+            for v in range(2):
+                cols = slice((2 * u + v) * P, (2 * u + v + 1) * P)
+                nc.tensor.matmul_mx(
+                    out=bank[:, v, :], lhsT=w2_wd[:, cols].bitcast(E5M2X4), lhsT_scale=w2_sd[:, cols],
+                    rhs=xo_wg[:].bitcast(E2M1X4), rhs_scale=xo_sg[:], start=True, stop=True,
+                )
+            pair = tile("b_sb%d" % u, [P, 2, J], F32)
+            nc.scalar.copy(pair[:], bank[:])
+            b_sb.extend([pair[:, 0, :], pair[:, 1, :]])
+
+        xt_wg = gathered("xt_wg", xt_w, l1, U32)
+        xt_sg = gathered("xt_sg", xt_s, l1, U8)
+        w_wd = dealt(nc.scalar.copy, "w_wd", w_w[:], U16, 8)
+        w_sd = dealt(nc.gpsimd.tensor_copy, "w_sd", w_s, U8, 16)
+        gate = tile("gate", [P, PACK, O], F32)
+        for t in range(PACK):
+            cols = slice(t * P, (t + 1) * P)
+            bank = ps.tile([P, J], F32, name="a_ps%d" % t)
+            nc.tensor.matmul_mx(
+                out=bank[:], lhsT=w_wd[:, cols].bitcast(E2M1X4), lhsT_scale=w_sd[:, cols],
+                rhs=xt_wg[:].bitcast(E4M3X4), rhs_scale=xt_sg[:], start=True, stop=True,
+            )
+            a_sb = tile("a_sb%d" % t, [P, J], F32)
+            nc.scalar.copy(a_sb[:], bank[:])
+            nc.scalar.activation(
+                out=gate[:, t, :], in_=a_sb[:].indirect(l4[:]), func=ACT.Sigmoid, scale=slope[:, t : t + 1]
+            )
+
+        b3 = tile("b3", [P, PACK, O], F32)
+        b4 = tile("b4", [P, PACK, O], F32)
+        for t in range(PACK):
+            nc.vector.tensor_copy(b3[:, t, :], b_sb[t].indirect(l3[:]))
+            nc.vector.tensor_copy(b4[:, t, :], b_sb[t].indirect(l4[:]))
+        larger = tile("larger", [P, PACK, O], F32)
+        nc.vector.tensor_tensor(larger[:], b3[:], b4[:], ALU.max)
+
+        p_ps = []
+        for h in range(2):
+            cols = slice(h * P, (h + 1) * P)
+            bank = ps.tile([P, O], F32, name="p_ps%d" % h)
+            nc.tensor.matmul_mx(
+                out=bank[:], lhsT=ws_w[:, cols].bitcast(E5M2X4), lhsT_scale=ws_s[:, cols],
+                rhs=sx_w[:].bitcast(E2M1X4), rhs_scale=sx_s, start=True, stop=False,
+            )
+            p_ps.append(bank)
+
+        hid = tile("hid", [P, O, PACK], BF16)
+        nc.vector.tensor_tensor(
+            hid[:], larger[:].rearrange("p t o -> p o t"), gate[:].rearrange("p t o -> p o t"), ALU.mult
+        )
+        hid_w = tile("hid_w", [P, O], U32)
+        hid_s = tile("hid_s", [P, O], U8)
+        nc.vector.quantize_mx(
+            out=hid_w[:].bitcast(E4M3X4), scales=hid_s[:], in_=hid[:].rearrange("p o t -> p (o t)")
+        )
+
+        tz_g = tile("tz_g", [P, 2, O], F32)
+        for h in range(2):
+            nc.scalar.activation(out=tz_g[:, h, :], in_=tz_sb[:, h, :].indirect(l5[:]), func=ACT.Copy)
+
+        for h, queue in enumerate((nc.sync, nc.scalar)):
+            cols = slice(h * P, (h + 1) * P)
+            nc.tensor.matmul_mx(
+                out=p_ps[h][:], lhsT=wb_w[:, cols].bitcast(E5M2X4), lhsT_scale=wb_s[:, cols],
+                rhs=hid_w[:].bitcast(E4M3X4), rhs_scale=hid_s[:], start=False, stop=True,
+            )
+            res = tile("res%d" % h, [P, O], F32)
+            nc.vector.tensor_tensor(res[:], p_ps[h][:], tz_g[:, h, :], ALU.add)
+            queue.dma_start(out[cols, :], res[:])

@@ -81,6 +81,10 @@ def tile_list_twotab_agree_skip_tabled_kernel(
         load_staged(nc.scalar, early, R, w_scales)
         load_scale_rows(nc.scalar, xo_s, xo_scales, 0)
         load_scale_rows(nc.scalar, xo_s, xo_scales, 1)
+        warm_in = tile("warm_in", [P, 1], F32)
+        warm_out = tile("warm_out", [P, 1], F32)
+        nc.vector.memset(warm_in[:], 0.0)
+        nc.scalar.activation(out=warm_out[:], in_=warm_in[:], func=ACT.Sigmoid)
         spread_staged(nc.scalar, early)
 
         l2 = load_list("l2", offs2)

@@ -67,33 +67,34 @@ def tile_list_twotab_agree_skip_tabled_kernel(
             queue.dma_start(plane[r:P:32, :].bitcast(I32), src[0, r:16:4, :].bitcast(I32))
 
         early = staged("early", 2 * R)
+        warm_in = tile("warm_in", [P, 1], F32)
+        warm_out = tile("warm_out", [P, 1], F32)
+        nc.vector.memset(warm_in[:], 0.0)
         xo_s = zeroed(nc.vector, "xo_s", Z)
-        xt_s = zeroed(nc.vector, "xt_s", T)
+        xt_s = zeroed(nc.gpsimd, "xt_s", T)
         late = staged("late", N + O + N)
         w2_s, w_s = early[:, 0, 0:R], early[:, 0, R : 2 * R]
         ws_s, sx_s, wb_s = late[:, 0, 0:N], late[:, 0, N : N + O], late[:, 0, N + O : N + O + N]
 
-        xt_w = load_words(nc.gpsimd, "xt_w", xt_words, T, U32)
         load_scale_rows(nc.gpsimd, xt_s, xt_scales, 2)
         load_scale_rows(nc.gpsimd, xt_s, xt_scales, 3)
+        load_staged(nc.gpsimd, late, N + O, wb_scales)
 
         load_staged(nc.scalar, early, 0, w2_scales)
         load_staged(nc.scalar, early, R, w_scales)
         load_scale_rows(nc.scalar, xo_s, xo_scales, 0)
-        load_scale_rows(nc.scalar, xo_s, xo_scales, 1)
-        warm_in = tile("warm_in", [P, 1], F32)
-        warm_out = tile("warm_out", [P, 1], F32)
-        nc.vector.memset(warm_in[:], 0.0)
         nc.scalar.activation(out=warm_out[:], in_=warm_in[:], func=ACT.Sigmoid)
-        spread_staged(nc.scalar, early)
 
         l2 = load_list("l2", offs2)
         xo_w = load_words(nc.sync, "xo_w", xo_words, Z, U16)
+        load_scale_rows(nc.sync, xo_s, xo_scales, 1)
+        w2_w = load_words(nc.sync, "w2_w", w2_words, R, U32)
+        xt_w = load_words(nc.sync, "xt_w", xt_words, T, U32)
         load_scale_rows(nc.sync, xo_s, xo_scales, 2)
         load_scale_rows(nc.sync, xo_s, xo_scales, 3)
-        w2_w = load_words(nc.sync, "w2_w", w2_words, R, U32)
-        l1 = load_list("l1", offs)
+        spread_staged(nc.sync, early)
         w_w = load_words(nc.sync, "w_w", w_words, R, U16)
+        l1 = load_list("l1", offs)
         load_scale_rows(nc.sync, xt_s, xt_scales, 0)
         load_scale_rows(nc.sync, xt_s, xt_scales, 1)
         l3 = load_list("l3", offs3)
@@ -102,13 +103,13 @@ def tile_list_twotab_agree_skip_tabled_kernel(
         nc.sync.dma_start(slope[:], sg.rearrange("(p t) o -> p (t o)", t=PACK))
         load_staged(nc.sync, late, 0, ws_scales)
         load_staged(nc.sync, late, N, sx_scales)
-        load_staged(nc.sync, late, N + O, wb_scales)
-        tz_sb = tile("tz_sb", [P, 2, E], F32)
-        nc.sync.dma_start(tz_sb[:], tz.rearrange("(h p) e -> p h e", p=P))
+        tz_sb = [tile("tz_sb%d" % h, [P, E], F32) for h in range(2)]
+        nc.sync.dma_start(tz_sb[0][:], tz[0:P, :])
         wb_w = load_words(nc.sync, "wb_w", wb_words, N, U32)
         ws_w = load_words(nc.sync, "ws_w", ws_words, N, U32)
         sx_w = load_words(nc.sync, "sx_w", sx_words, O, U16)
         l5 = load_list("l5", offs5)
+        nc.sync.dma_start(tz_sb[1][:], tz[P : 2 * P, :])
         spread_staged(nc.sync, late)
 
         def dealt(copy, name, src, dtype, run):
@@ -127,24 +128,23 @@ def tile_list_twotab_agree_skip_tabled_kernel(
         xo_wg = gathered("xo_wg", xo_w, l2, U16)
         xo_sg = gathered("xo_sg", xo_s, l2, U8)
         w2_wd = dealt(nc.scalar.copy, "w2_wd", w2_w[:], U32, 4)
-        w2_sd = dealt(nc.gpsimd.tensor_copy, "w2_sd", w2_s, U8, 16)
+        w2_sd = dealt(nc.vector.tensor_copy, "w2_sd", w2_s, U8, 16)
         b_sb = []
-        for u in range(2):
-            bank = ps.tile([P, 2, J], F32, name="b_ps%d" % u)
-            for v in range(2):
-                cols = slice((2 * u + v) * P, (2 * u + v + 1) * P)
-                nc.tensor.matmul_mx(
-                    out=bank[:, v, :], lhsT=w2_wd[:, cols].bitcast(E5M2X4), lhsT_scale=w2_sd[:, cols],
-                    rhs=xo_wg[:].bitcast(E2M1X4), rhs_scale=xo_sg[:], start=True, stop=True,
-                )
-            pair = tile("b_sb%d" % u, [P, 2, J], F32)
-            nc.scalar.copy(pair[:], bank[:])
-            b_sb.extend([pair[:, 0, :], pair[:, 1, :]])
+        for t in range(PACK):
+            cols = slice(t * P, (t + 1) * P)
+            bank = ps.tile([P, J], F32, name="b_ps%d" % t, tag="bank%d" % t)
+            nc.tensor.matmul_mx(
+                out=bank[:], lhsT=w2_wd[:, cols].bitcast(E5M2X4), lhsT_scale=w2_sd[:, cols],
+                rhs=xo_wg[:].bitcast(E2M1X4), rhs_scale=xo_sg[:], start=True, stop=True,
+            )
+            rows = tile("b_sb%d" % t, [P, J], F32)
+            nc.scalar.copy(rows[:], bank[:])
+            b_sb.append(rows)
 
         xt_wg = gathered("xt_wg", xt_w, l1, U32)
         xt_sg = gathered("xt_sg", xt_s, l1, U8)
         w_wd = dealt(nc.scalar.copy, "w_wd", w_w[:], U16, 8)
-        w_sd = dealt(nc.gpsimd.tensor_copy, "w_sd", w_s, U8, 16)
+        w_sd = dealt(nc.vector.tensor_copy, "w_sd", w_s, U8, 16)
         gate = tile("gate", [P, PACK, O], F32)
         for t in range(PACK):
             cols = slice(t * P, (t + 1) * P)
@@ -162,15 +162,15 @@ def tile_list_twotab_agree_skip_tabled_kernel(
         b3 = tile("b3", [P, PACK, O], F32)
         b4 = tile("b4", [P, PACK, O], F32)
         for t in range(PACK):
-            nc.vector.tensor_copy(b3[:, t, :], b_sb[t].indirect(l3[:]))
-            nc.vector.tensor_copy(b4[:, t, :], b_sb[t].indirect(l4[:]))
+            nc.vector.tensor_copy(b3[:, t, :], b_sb[t][:].indirect(l3[:]))
+            nc.vector.tensor_copy(b4[:, t, :], b_sb[t][:].indirect(l4[:]))
         larger = tile("larger", [P, PACK, O], F32)
         nc.vector.tensor_tensor(larger[:], b3[:], b4[:], ALU.max)
 
         p_ps = []
         for h in range(2):
             cols = slice(h * P, (h + 1) * P)
-            bank = ps.tile([P, O], F32, name="p_ps%d" % h)
+            bank = ps.tile([P, O], F32, name="p_ps%d" % h, tag="bank%d" % h)
             nc.tensor.matmul_mx(
                 out=bank[:], lhsT=ws_w[:, cols].bitcast(E5M2X4), lhsT_scale=ws_s[:, cols],
                 rhs=sx_w[:].bitcast(E2M1X4), rhs_scale=sx_s, start=True, stop=False,
@@ -179,7 +179,10 @@ def tile_list_twotab_agree_skip_tabled_kernel(
 
         hid = tile("hid", [P, O, PACK], BF16)
         nc.vector.tensor_tensor(
-            hid[:], larger[:].rearrange("p t o -> p o t"), gate[:].rearrange("p t o -> p o t"), ALU.mult
+            hid[:].rearrange("p (c i) t -> p c t i", i=4),
+            larger[:].rearrange("p t (c i) -> p c t i", i=4),
+            gate[:].rearrange("p t (c i) -> p c t i", i=4),
+            ALU.mult,
         )
         hid_w = tile("hid_w", [P, O], U32)
         hid_s = tile("hid_s", [P, O], U8)
@@ -189,7 +192,7 @@ def tile_list_twotab_agree_skip_tabled_kernel(
 
         tz_g = tile("tz_g", [P, 2, O], F32)
         for h in range(2):
-            nc.scalar.activation(out=tz_g[:, h, :], in_=tz_sb[:, h, :].indirect(l5[:]), func=ACT.Copy)
+            nc.scalar.activation(out=tz_g[:, h, :], in_=tz_sb[h][:].indirect(l5[:]), func=ACT.Copy)
 
         for h, queue in enumerate((nc.sync, nc.scalar)):
             cols = slice(h * P, (h + 1) * P)

from contextlib import ExitStack

import concourse.mybir as mybir

F32 = mybir.dt.float32
BF16 = mybir.dt.bfloat16
I32 = mybir.dt.int32
U32 = mybir.dt.uint32
U16 = mybir.dt.uint16
U8 = mybir.dt.uint8
E4M3X4 = mybir.dt.float8_e4m3fn_x4
E5M2X4 = mybir.dt.float8_e5m2_x4
E2M1X4 = mybir.dt.float4_e2m1fn_x4
ACT = mybir.ActivationFunctionType
ALU = mybir.AluOpType

P = 128
PACK = 4
T, Z, J, R, O, N, E = 1024, 1024, 256, 512, 128, 256, 1024
FLOPS = 2 * 512 * (R * J * 2 + N * O * 2)


def tile_list_twotab_agree_skip_tabled_kernel(
    tc, xt_words, xt_scales, w_words, w_scales, xo_words, xo_scales, w2_words, w2_scales, sg,
    wb_words, wb_scales, sx_words, sx_scales, ws_words, ws_scales, tz, offs, offs2, offs3, offs4, offs5, out,
):
    nc = tc.nc
    with ExitStack() as ctx:
        sb = ctx.enter_context(tc.tile_pool(name="sb", bufs=1))
        ps = ctx.enter_context(tc.psum_pool(name="ps", bufs=1))

        def tile(name, shape, dtype):
            return sb.tile(shape, dtype, name=name, align_bytes=64)

        def load_list(name, src):
            held = tile(name, list(src.shape), U16)
            nc.sync.dma_start(held[:], src)
            return held

        def load_words(queue, name, src, cols, dtype):
            held = tile(name, [P, cols], dtype)
            flat = src[0] if len(src.shape) == 3 else src[0].rearrange("p n t -> p (n t)")
            queue.dma_start(held[:].bitcast(I32), flat.bitcast(I32))
            return held

        def zeroed(engine, name, cols):
            plane = tile(name, [P, cols], U8)
            engine.memset(plane[:].bitcast(I32), 0)
            return plane

        def staged(name, cols):
            held = tile(name, [P, 4, cols], U8)
            nc.vector.memset(held[:, 0, :].bitcast(I32), 0)
            return held

        def load_staged(queue, held, first, src):
            queue.dma_start(
                held[0:P:32, :, first : first + src.shape[2]].bitcast(I32),
                src[0].rearrange("(q r) c -> q r c", r=4).bitcast(I32),
            )

        def spread_staged(queue, held):
            for r in range(1, 4):
                queue.dma_start(held[r:P:32, 0, :].bitcast(I32), held[0:P:32, r, :].bitcast(I32))

        def load_scale_rows(queue, plane, src, r):
            queue.dma_start(plane[r:P:32, :].bitcast(I32), src[0, r:16:4, :].bitcast(I32))

        early = staged("early", 2 * R)
        warm_in = tile("warm_in", [P, 1], F32)
        warm_out = tile("warm_out", [P, 1], F32)
        nc.vector.memset(warm_in[:], 0.0)
        xo_s = zeroed(nc.vector, "xo_s", Z)
        xt_s = zeroed(nc.gpsimd, "xt_s", T)
        late = staged("late", N + O + N)
        w2_s, w_s = early[:, 0, 0:R], early[:, 0, R : 2 * R]
        ws_s, sx_s, wb_s = late[:, 0, 0:N], late[:, 0, N : N + O], late[:, 0, N + O : N + O + N]

        load_scale_rows(nc.gpsimd, xt_s, xt_scales, 2)
        load_scale_rows(nc.gpsimd, xt_s, xt_scales, 3)
        load_staged(nc.gpsimd, late, N + O, wb_scales)

        load_staged(nc.scalar, early, 0, w2_scales)
        load_staged(nc.scalar, early, R, w_scales)
        load_scale_rows(nc.scalar, xo_s, xo_scales, 0)
        nc.scalar.activation(out=warm_out[:], in_=warm_in[:], func=ACT.Sigmoid)

        l2 = load_list("l2", offs2)
        xo_w = load_words(nc.sync, "xo_w", xo_words, Z, U16)
        load_scale_rows(nc.sync, xo_s, xo_scales, 1)
        w2_w = load_words(nc.sync, "w2_w", w2_words, R, U32)
        xt_w = load_words(nc.sync, "xt_w", xt_words, T, U32)
        load_scale_rows(nc.sync, xo_s, xo_scales, 2)
        load_scale_rows(nc.sync, xo_s, xo_scales, 3)
        spread_staged(nc.sync, early)
        w_w = load_words(nc.sync, "w_w", w_words, R, U16)
        l1 = load_list("l1", offs)
        load_scale_rows(nc.sync, xt_s, xt_scales, 0)
        load_scale_rows(nc.sync, xt_s, xt_scales, 1)
        l3 = load_list("l3", offs3)
        l4 = load_list("l4", offs4)
        slope = tile("slope", [P, PACK], F32)
        nc.sync.dma_start(slope[:], sg.rearrange("(p t) o -> p (t o)", t=PACK))
        load_staged(nc.sync, late, 0, ws_scales)
        load_staged(nc.sync, late, N, sx_scales)
        tz_sb = [tile("tz_sb%d" % h, [P, E], F32) for h in range(2)]
        nc.sync.dma_start(tz_sb[0][:], tz[0:P, :])
        wb_w = load_words(nc.sync, "wb_w", wb_words, N, U32)
        ws_w = load_words(nc.sync, "ws_w", ws_words, N, U32)
        sx_w = load_words(nc.sync, "sx_w", sx_words, O, U16)
        l5 = load_list("l5", offs5)
        nc.sync.dma_start(tz_sb[1][:], tz[P : 2 * P, :])
        spread_staged(nc.sync, late)

        def dealt(copy, name, src, dtype, run):
            held = tile(name, [P, R], dtype)
            copy(
                held[:].rearrange("p (t c i) -> p c t i", t=PACK, i=run),
                src.rearrange("p (c i t) -> p c t i", t=PACK, i=run),
            )
            return held

        def gathered(name, window, offsets, dtype):
            held = tile(name, [P, J], dtype)
            nc.vector.tensor_copy(held[:], window[:].indirect(offsets[:]))
            return held

        xo_wg = gathered("xo_wg", xo_w, l2, U16)
        xo_sg = gathered("xo_sg", xo_s, l2, U8)
        w2_wd = dealt(nc.scalar.copy, "w2_wd", w2_w[:], U32, 4)
        w2_sd = dealt(nc.vector.tensor_copy, "w2_sd", w2_s, U8, 16)
        b_sb = []
        for t in range(PACK):
            cols = slice(t * P, (t + 1) * P)
            bank = ps.tile([P, J], F32, name="b_ps%d" % t, tag="bank%d" % t)
            nc.tensor.matmul_mx(
                out=bank[:], lhsT=w2_wd[:, cols].bitcast(E5M2X4), lhsT_scale=w2_sd[:, cols],
                rhs=xo_wg[:].bitcast(E2M1X4), rhs_scale=xo_sg[:], start=True, stop=True,
            )
            rows = tile("b_sb%d" % t, [P, J], F32)
            nc.scalar.copy(rows[:], bank[:])
            b_sb.append(rows)

        xt_wg = gathered("xt_wg", xt_w, l1, U32)
        xt_sg = gathered("xt_sg", xt_s, l1, U8)
        w_wd = dealt(nc.scalar.copy, "w_wd", w_w[:], U16, 8)
        w_sd = dealt(nc.vector.tensor_copy, "w_sd", w_s, U8, 16)
        gate = tile("gate", [P, PACK, O], F32)
        for t in range(PACK):
            cols = slice(t * P, (t + 1) * P)
            bank = ps.tile([P, J], F32, name="a_ps%d" % t)
            nc.tensor.matmul_mx(
                out=bank[:], lhsT=w_wd[:, cols].bitcast(E2M1X4), lhsT_scale=w_sd[:, cols],
                rhs=xt_wg[:].bitcast(E4M3X4), rhs_scale=xt_sg[:], start=True, stop=True,
            )
            a_sb = tile("a_sb%d" % t, [P, J], F32)
            nc.scalar.copy(a_sb[:], bank[:])
            nc.scalar.activation(
                out=gate[:, t, :], in_=a_sb[:].indirect(l4[:]), func=ACT.Sigmoid, scale=slope[:, t : t + 1]
            )

        b3 = tile("b3", [P, PACK, O], F32)
        b4 = tile("b4", [P, PACK, O], F32)
        for t in range(PACK):
            nc.vector.tensor_copy(b3[:, t, :], b_sb[t][:].indirect(l3[:]))
            nc.vector.tensor_copy(b4[:, t, :], b_sb[t][:].indirect(l4[:]))
        larger = tile("larger", [P, PACK, O], F32)
        nc.vector.tensor_tensor(larger[:], b3[:], b4[:], ALU.max)

        p_ps = []
        for h in range(2):
            cols = slice(h * P, (h + 1) * P)
            bank = ps.tile([P, O], F32, name="p_ps%d" % h, tag="bank%d" % h)
            nc.tensor.matmul_mx(
                out=bank[:], lhsT=ws_w[:, cols].bitcast(E5M2X4), lhsT_scale=ws_s[:, cols],
                rhs=sx_w[:].bitcast(E2M1X4), rhs_scale=sx_s, start=True, stop=False,
            )
            p_ps.append(bank)

        hid = tile("hid", [P, O, PACK], BF16)
        nc.vector.tensor_tensor(
            hid[:].rearrange("p (c i) t -> p c t i", i=4),
            larger[:].rearrange("p t (c i) -> p c t i", i=4),
            gate[:].rearrange("p t (c i) -> p c t i", i=4),
            ALU.mult,
        )
        hid_w = tile("hid_w", [P, O], U32)
        hid_s = tile("hid_s", [P, O], U8)
        nc.vector.quantize_mx(
            out=hid_w[:].bitcast(E4M3X4), scales=hid_s[:], in_=hid[:].rearrange("p o t -> p (o t)")
        )

        tz_g = tile("tz_g", [P, 2, O], F32)
        for h in range(2):
            nc.scalar.activation(out=tz_g[:, h, :], in_=tz_sb[h][:].indirect(l5[:]), func=ACT.Copy)

        for h, queue in enumerate((nc.sync, nc.scalar)):
            cols = slice(h * P, (h + 1) * P)
            nc.tensor.matmul_mx(
                out=p_ps[h][:], lhsT=wb_w[:, cols].bitcast(E5M2X4), lhsT_scale=wb_s[:, cols],
                rhs=hid_w[:].bitcast(E4M3X4), rhs_scale=hid_s[:], start=False, stop=True,
            )
            res = tile("res%d" % h, [P, O], F32)
            nc.vector.tensor_tensor(res[:], p_ps[h][:], tz_g[:, h, :], ALU.add)
            queue.dma_start(out[cols, :], res[:])
